import numpy as np
import ml_dtypes


def mxq(x, axis, fmt="e4m3"):
    dtype, down = {"e4m3": (ml_dtypes.float8_e4m3fn, 7), "e5m2": (ml_dtypes.float8_e5m2, 14)}[fmt]
    v = np.moveaxis(np.asarray(x, np.float32).astype(ml_dtypes.bfloat16).astype(np.float64), axis, -1)
    blocks = v.reshape(v.shape[:-1] + (-1, 32))
    amax = np.abs(blocks).max(-1, keepdims=True)
    byte = np.maximum(np.where(amax > 0, np.frexp(amax)[1] - 1 + 127, 0) - down, 1)
    scale = np.exp2(byte - 127.0)
    codes = (blocks / scale).astype(np.float32).astype(dtype).astype(np.float64)
    return np.moveaxis((codes * scale).reshape(v.shape), -1, axis)


WIDE = False


def mx_kscale(k):
    if not WIDE:
        return np.ones(k)
    levels = np.array([10, -10, 5, -5, 0])
    if k % 512:
        return np.exp2(np.random.permutation(np.resize(levels, k // 32))).repeat(32)
    a = np.empty((k // 512, 16))
    for p in range(k // 512):
        a[p, :8] = np.random.permutation(np.resize(levels, 8))
        for g in range(8):
            far = levels[np.abs(levels - a[p, g]) >= 10]
            a[p, g + 8] = far[np.random.randint(len(far))]
    return np.exp2(a.ravel()).repeat(32)


def f64(x):
    return np.asarray(x).astype(np.float64)


def striped(idx):
    return np.tile(idx.reshape(-1, 16).T, (8, 1)).astype(np.uint16)


def unstriped(offs):
    return offs[:16].T.reshape(-1).astype(np.int64)


def striped8(idx):
    return np.concatenate([x.reshape(-1, 16).T for x in idx]).astype(np.uint16)


def runs(offs, k):
    lists = np.stack([offs[16 * r : 16 * r + 16].T.reshape(-1) for r in range(8)]).astype(np.int64)
    return lists[np.arange(k) % 512 // 64]


def pack_weight(w):
    k, n = w.shape
    w = f64(np.asarray(w, np.float32).astype(ml_dtypes.bfloat16)).reshape(k // 32, 32, n)
    amax = np.abs(w).max(1)
    byte = np.clip(np.where(amax > 0, np.frexp(amax)[1] - 1 + 127 - 7, 1), 1, 254)
    scaled = (w * np.exp2(127.0 - byte)[:, None, :]).reshape(k, n).astype(np.float32)
    words = np.ascontiguousarray(scaled.reshape(k // 512, 128, 4, n).transpose(0, 1, 3, 2)).astype(ml_dtypes.float8_e4m3fn).view(np.uint8)
    return words, np.ascontiguousarray(byte.astype(np.uint8).reshape(k // 512, 16, n))


def unpack_weight(words, scales):
    g, p, n, _ = words.shape
    vals = np.ascontiguousarray(words).view(ml_dtypes.float8_e4m3fn).astype(np.float64) * np.repeat(np.exp2(scales.astype(np.float64) - 127.0), 8, axis=1)[..., None]
    return vals.transpose(0, 1, 3, 2).reshape(g * 512, n)


def sigmoid(v):
    return 1.0 / (1.0 + np.exp(-np.maximum(v, -700.0)))


K, T, S, H, C = 512, 2048, 512, 512, 512


def setup_inputs():
    n = np.random.standard_normal
    s = mx_kscale(K)[:, None]
    packed_xT = pack_weight(n((K, T)) * s)
    return {
        "x_words": packed_xT[0],
        "x_scales": packed_xT[1],
        "w1": (n((K, H)) / np.sqrt(K) / s).astype(np.float32),
        "gs": (np.random.uniform(0.5, 1.5, (K, 1)) / s).astype(np.float32),
        "offs": striped(np.random.permutation(T)[:S]),
        "n1": striped8(np.stack([np.random.permutation(S) for _ in range(8)])),
        "ca": striped(np.random.permutation(T)[:C]),
        "cb": striped(np.random.permutation(T)[:C]),
        "n2": striped8(np.stack([np.random.permutation(S) for _ in range(8)])),
        "n3": striped8(np.stack([np.random.permutation(S) for _ in range(8)])),
    }


def reference(x_words, x_scales, w1, gs, offs, n1, ca, cb, n2, n3):
    x_ca = unpack_weight(x_words, x_scales)[:, unstriped(ca)]
    xq = unpack_weight(x_words, x_scales)[:, unstriped(offs)]
    y = mxq(f64(w1), 0, "e4m3").T @ xq
    st = y * (sigmoid(y[np.arange(H)[:, None], runs(n1, H)]))
    z = f64(gs) * (np.maximum(st, st[np.arange(H)[:, None], runs(n1, H)]))
    zq = mxq(z, 0, "e4m3")
    a = 0.0625 * (x_ca.T @ zq)
    x_cb = unpack_weight(x_words, x_scales)[:, unstriped(cb)]
    b = 0.0625 * (x_cb.T @ zq)
    return np.maximum(a, b[np.arange(C)[:, None], runs(n3, C)]) - (np.minimum(a[np.arange(C)[:, None], runs(n2, C)], b))

@@ -1,0 +1,202 @@
+from contextlib import ExitStack
+
+import concourse.mybir as mybir
+
+K, T, S, H, C = 512, 2048, 512, 512, 512
+FLOPS = 3 * 2 * 512 * 512 * 512
+
+F32 = mybir.dt.float32
+BF16 = mybir.dt.bfloat16
+I32 = mybir.dt.int32
+U32 = mybir.dt.uint32
+U16 = mybir.dt.uint16
+U8 = mybir.dt.uint8
+FP8X4 = mybir.dt.float8_e4m3fn_x4
+ALU = mybir.AluOpType
+ACT = mybir.ActivationFunctionType
+
+P = 128
+PACK = 4
+LANES = 16
+HALVES = ((0, 256), (256, 512))
+Z_CHUNKS = ((0, 256), (256, 384), (384, 512))
+SIXTEENTH = 0.0625
+
+
+def tile_picked_ccmpmaxbtwicp_none_p_kernel(
+    tc, x_words, x_scales, w1, gs, offs, n1, ca, cb, n2, n3, out
+):
+    nc = tc.nc
+    with ExitStack() as ctx:
+        lists = ctx.enter_context(tc.tile_pool(name="lists", bufs=1))
+        sb = ctx.enter_context(tc.tile_pool(name="sb", bufs=1))
+        psum = ctx.enter_context(tc.psum_pool(name="psum", bufs=1))
+
+        def load_list(name, src):
+            tile = lists.tile([P, S // LANES], U16, name=name)
+            nc.sync.dma_start(tile[:], src)
+            return tile
+
+        def entries(tile, lo, hi):
+            return tile[:, lo // LANES : hi // LANES]
+
+        x_plane = sb.tile([P, T], U8, name="x_plane", align_bytes=64)
+        nc.vector.memset(x_plane[:].bitcast(I32), 0)
+        for q in range(4):
+            nc.scalar.dma_start(
+                x_plane[32 * q : 32 * q + 4, :].bitcast(I32), x_scales[0, 4 * q : 4 * q + 4, :].bitcast(I32)
+            )
+        offs_sb = load_list("offs_sb", offs)
+        x_codes = sb.tile([P, T], U32, name="x_codes", align_bytes=64)
+        nc.sync.dma_start(x_codes[:].bitcast(I32), x_words[0].rearrange("p n t -> p (n t)").bitcast(I32))
+        ca_sb = load_list("ca_sb", ca)
+        w_rows = w1.rearrange("(p j) c -> p j c", j=PACK)
+        w_raw = []
+        for h, (lo, hi) in enumerate(HALVES):
+            raw = sb.tile([P, PACK, hi - lo], F32, name="w_raw%d" % h, tag="w_raw%d" % h, align_bytes=64)
+            nc.sync.dma_start(raw[:], w_rows[:, :, lo:hi])
+            w_raw.append(raw)
+        cb_sb = load_list("cb_sb", cb)
+        n1_sb = load_list("n1_sb", n1)
+        gs_sb = sb.tile([P, PACK], F32, name="gs_sb")
+        nc.sync.dma_start(gs_sb[:], gs.rearrange("(p t) one -> p (t one)", t=PACK))
+        n3_sb = load_list("n3_sb", n3)
+        n2_sb = load_list("n2_sb", n2)
+
+        def pick_scales(name, list_sb, tag):
+            picked = sb.tile([P, S], U8, name=name, tag=tag, align_bytes=64)
+            nc.vector.tensor_copy(picked[:], x_plane[:].indirect(list_sb[:]))
+            return picked
+
+        def deal_scales(name, picked):
+            dealt = sb.tile([P, S], U8, name=name, align_bytes=64)
+            nc.vector.tensor_copy(
+                dealt[:].rearrange("p (t m) -> p t m", t=PACK), picked[:].rearrange("p (m t) -> p t m", t=PACK)
+            )
+            return dealt
+
+        def pick_dealt_codes(name, list_sb, tag):
+            dealt = sb.tile([P, S], U32, name=name, tag=tag, align_bytes=64)
+            nc.vector.tensor_copy(dealt[:].rearrange("p (t m) -> p m t", t=PACK), x_codes[:].indirect(list_sb[:]))
+            return dealt
+
+        xq_codes = sb.tile([P, S], U32, name="xq_codes", align_bytes=64)
+        nc.vector.tensor_copy(xq_codes[:], x_codes[:].indirect(offs_sb[:]))
+        xq_scales = pick_scales("xq_scales", offs_sb, "xq_scales")
+        ca_picked = pick_scales("ca_picked", ca_sb, "ca_picked")
+
+        w_bf = sb.tile([P, PACK, P, PACK], BF16, name="w_bf", tag="w_bf", align_bytes=64)
+        for h, (lo, hi) in enumerate(HALVES):
+            src = w_raw[h][:].rearrange("p j (m t) -> p m t j", t=PACK)
+            dst = w_bf[:, :, lo // PACK : hi // PACK, :].rearrange("p t m j -> p m t j")
+            nc.scalar.copy(dst, src)
+        w_codes = sb.tile([P, H], U32, name="w_codes", align_bytes=64)
+        w_scales = sb.tile([P, H], U8, name="w_scales", align_bytes=64)
+        y_ps = []
+        for t in range(PACK):
+            cols = slice(t * P, (t + 1) * P)
+            nc.vector.quantize_mx(
+                w_codes[:, cols].bitcast(FP8X4), w_scales[:, cols], w_bf[:, t].rearrange("p m j -> p (m j)")
+            )
+            bank = psum.tile([P, S], F32, name="y_ps%d" % t, tag="bank%d" % (4 + t))
+            nc.tensor.matmul_mx(
+                bank[:], w_codes[:, cols].bitcast(FP8X4), w_scales[:, cols],
+                xq_codes[:].bitcast(FP8X4), xq_scales[:], start=True, stop=True,
+            )
+            y_ps.append(bank)
+
+        ca_codes = pick_dealt_codes("ca_codes", ca_sb, "w_bf")
+        ca_scales = deal_scales("ca_scales", ca_picked)
+        cb_scales = deal_scales("cb_scales", pick_scales("cb_picked", cb_sb, "w_raw1"))
+
+        z_rows = [sb.tile([P, PACK, hi - lo], BF16, name="z_rows%d" % c) for c, (lo, hi) in enumerate(Z_CHUNKS)]
+        st = []
+
+        larger_of = {}
+
+        def scale(t, c):
+            nc.scalar.activation(z_rows[c][:, t, :], larger_of[t, c][:], ACT.Copy, scale=gs_sb[:, t : t + 1])
+
+        def larger_scaled(t, c):
+            lo, hi = Z_CHUNKS[c]
+            fetched = sb.tile([P, hi - lo], F32, name="st_n1_%d_%d" % (t, c), tag="st_n1_%d_%d" % (t, c), align_bytes=64)
+            nc.vector.tensor_copy(fetched[:], st[t][:].indirect(entries(n1_sb, lo, hi)))
+            larger = sb.tile([P, hi - lo], F32, name="larger_%d_%d" % (t, c))
+            nc.vector.tensor_tensor(larger[:], fetched[:], st[t][:, lo:hi], ALU.max)
+            larger_of[t, c] = larger
+
+        gates = []
+        for t in range(PACK):
+            y_sb = sb.tile([P, S], F32, name="y_sb%d" % t)
+            nc.scalar.copy(y_sb[:], y_ps[t][:])
+            gate = sb.tile([P, S], F32, name="gate%d" % t)
+            for lo, hi in HALVES:
+                nc.scalar.activation(gate[:, lo:hi], y_sb[:].indirect(entries(n1_sb, lo, hi)), ACT.Sigmoid)
+            gates.append(gate)
+        for t in range(PACK):
+            st_t = sb.tile([P, S], F32, name="st%d" % t)
+            nc.vector.tensor_tensor(st_t[:], y_ps[t][:], gates[t][:], ALU.mult)
+            st.append(st_t)
+            larger_scaled(t, 0)
+
+        z_codes = sb.tile([P, S], U32, name="z_codes", align_bytes=64)
+        z_scales = sb.tile([P, S], U8, name="z_scales", align_bytes=64)
+
+        def quantize_z(c):
+            lo, hi = Z_CHUNKS[c]
+            woven = sb.tile([P, (hi - lo) * PACK], BF16, name="z_woven%d" % c, align_bytes=64)
+            nc.scalar.copy(
+                woven[:].rearrange("p (g i t) -> p g t i", i=4, t=PACK),
+                z_rows[c][:].rearrange("p t (g i) -> p g t i", i=4),
+            )
+            nc.vector.quantize_mx(z_codes[:, lo:hi].bitcast(FP8X4), z_scales[:, lo:hi], woven[:])
+
+        a_ps = [psum.tile([P, S], F32, name="a_ps%d" % t, tag="bank%d" % (2 * t)) for t in range(PACK)]
+        b_ps = [psum.tile([P, S], F32, name="b_ps%d" % t, tag="bank%d" % (2 * t + 1)) for t in range(PACK)]
+        a_sb = [sb.tile([P, S], F32, name="a_sb%d" % t) for t in range(PACK)]
+        b_sb = [sb.tile([P, S], F32, name="b_sb%d" % t) for t in range(PACK)]
+
+        def score(bank, window, codes, scales, t, lo, hi):
+            cols = slice(t * P, (t + 1) * P)
+            nc.tensor.matmul_mx(
+                bank[:, lo:hi], codes[:, cols].bitcast(FP8X4), scales[:, cols],
+                z_codes[:, lo:hi].bitcast(FP8X4), z_scales[:, lo:hi], start=True, stop=True,
+            )
+            nc.scalar.activation(window[:, lo:hi], bank[:, lo:hi], ACT.Copy, scale=SIXTEENTH)
+
+        for c, (lo, hi) in enumerate(Z_CHUNKS):
+            if c > 0:
+                for t in range(PACK):
+                    larger_scaled(t, c)
+            for t in range(PACK):
+                scale(t, c)
+            quantize_z(c)
+            score(a_ps[0], a_sb[0], ca_codes, ca_scales, 0, lo, hi)
+        cb_codes = pick_dealt_codes("cb_codes", cb_sb, "st_n1_3_2")
+        score(b_ps[0], b_sb[0], cb_codes, cb_scales, 0, 0, S)
+        for t in range(1, PACK):
+            score(a_ps[t], a_sb[t], ca_codes, ca_scales, t, 0, S)
+            score(b_ps[t], b_sb[t], cb_codes, cb_scales, t, 0, S)
+
+        out_rows = out.rearrange("(p t) j -> p t j", t=PACK)
+        for t in range(PACK):
+            a_n2 = sb.tile([P, S], F32, name="a_n2_%d" % t)
+            b_n3 = sb.tile([P, S], F32, name="b_n3_%d" % t)
+            upper = sb.tile([P, S], F32, name="upper%d" % t)
+            lower = sb.tile([P, S], F32, name="lower%d" % t)
+            result = sb.tile([P, S], F32, name="result%d" % t)
+            last = t == PACK - 1
+            for lo, hi in HALVES:
+                nc.vector.tensor_copy(a_n2[:, lo:hi], a_sb[t][:].indirect(entries(n2_sb, lo, hi)))
+                nc.vector.tensor_copy(b_n3[:, lo:hi], b_sb[t][:].indirect(entries(n3_sb, lo, hi)))
+                if last or hi == S:
+                    c0 = lo if last else 0
+                    nc.vector.scalar_tensor_tensor(
+                        lower[:, c0:hi], b_ps[t][:, c0:hi], SIXTEENTH, a_n2[:, c0:hi], ALU.mult, ALU.min
+                    )
+                    nc.vector.scalar_tensor_tensor(
+                        upper[:, c0:hi], a_ps[t][:, c0:hi], SIXTEENTH, b_n3[:, c0:hi], ALU.mult, ALU.max
+                    )
+                    engine = nc.vector if (last and hi == S) else nc.gpsimd
+                    engine.tensor_tensor(result[:, c0:hi], upper[:, c0:hi], lower[:, c0:hi], ALU.subtract)
+                    nc.sync.dma_start(out_rows[:, t, c0:hi], result[:, c0:hi])

@@ -46,6 +46,9 @@ def tile_picked_ccmpmaxbtwicp_none_p_kernel(
             nc.scalar.dma_start(
                 x_plane[32 * q : 32 * q + 4, :].bitcast(I32), x_scales[0, 4 * q : 4 * q + 4, :].bitcast(I32)
             )
+        warm = sb.tile([P, 8], F32, name="warm")
+        nc.vector.memset(warm[:], 0.0)
+        nc.scalar.activation(warm[:, 1:2], warm[:, 0:1], ACT.Sigmoid)
         offs_sb = load_list("offs_sb", offs)
         x_codes = sb.tile([P, T], U32, name="x_codes", align_bytes=64)
         nc.sync.dma_start(x_codes[:].bitcast(I32), x_words[0].rearrange("p n t -> p (n t)").bitcast(I32))
@@ -68,8 +71,8 @@ def tile_picked_ccmpmaxbtwicp_none_p_kernel(
             nc.vector.tensor_copy(picked[:], x_plane[:].indirect(list_sb[:]))
             return picked
 
-        def deal_scales(name, picked):
-            dealt = sb.tile([P, S], U8, name=name, align_bytes=64)
+        def deal_scales(name, picked, tag):
+            dealt = sb.tile([P, S], U8, name=name, tag=tag, align_bytes=64)
             nc.vector.tensor_copy(
                 dealt[:].rearrange("p (t m) -> p t m", t=PACK), picked[:].rearrange("p (m t) -> p t m", t=PACK)
             )
@@ -90,40 +93,19 @@ def tile_picked_ccmpmaxbtwicp_none_p_kernel(
             src = w_raw[h][:].rearrange("p j (m t) -> p m t j", t=PACK)
             dst = w_bf[:, :, lo // PACK : hi // PACK, :].rearrange("p t m j -> p m t j")
             nc.scalar.copy(dst, src)
-        w_codes = sb.tile([P, H], U32, name="w_codes", align_bytes=64)
-        w_scales = sb.tile([P, H], U8, name="w_scales", align_bytes=64)
         y_ps = []
         for t in range(PACK):
-            cols = slice(t * P, (t + 1) * P)
-            nc.vector.quantize_mx(
-                w_codes[:, cols].bitcast(FP8X4), w_scales[:, cols], w_bf[:, t].rearrange("p m j -> p (m j)")
-            )
+            w_codes = sb.tile([P, P], U32, name="w_codes%d" % t, tag="w_codes%d" % t, align_bytes=64)
+            w_scales = sb.tile([P, P], U8, name="w_scales%d" % t, align_bytes=64)
+            nc.vector.quantize_mx(w_codes[:].bitcast(FP8X4), w_scales[:], w_bf[:, t].rearrange("p m j -> p (m j)"))
             bank = psum.tile([P, S], F32, name="y_ps%d" % t, tag="bank%d" % (4 + t))
             nc.tensor.matmul_mx(
-                bank[:], w_codes[:, cols].bitcast(FP8X4), w_scales[:, cols],
+                bank[:], w_codes[:].bitcast(FP8X4), w_scales[:],
                 xq_codes[:].bitcast(FP8X4), xq_scales[:], start=True, stop=True,
             )
             y_ps.append(bank)
 
         ca_codes = pick_dealt_codes("ca_codes", ca_sb, "w_bf")
-        ca_scales = deal_scales("ca_scales", ca_picked)
-        cb_scales = deal_scales("cb_scales", pick_scales("cb_picked", cb_sb, "w_raw1"))
-
-        z_rows = [sb.tile([P, PACK, hi - lo], BF16, name="z_rows%d" % c) for c, (lo, hi) in enumerate(Z_CHUNKS)]
-        st = []
-
-        larger_of = {}
-
-        def scale(t, c):
-            nc.scalar.activation(z_rows[c][:, t, :], larger_of[t, c][:], ACT.Copy, scale=gs_sb[:, t : t + 1])
-
-        def larger_scaled(t, c):
-            lo, hi = Z_CHUNKS[c]
-            fetched = sb.tile([P, hi - lo], F32, name="st_n1_%d_%d" % (t, c), tag="st_n1_%d_%d" % (t, c), align_bytes=64)
-            nc.vector.tensor_copy(fetched[:], st[t][:].indirect(entries(n1_sb, lo, hi)))
-            larger = sb.tile([P, hi - lo], F32, name="larger_%d_%d" % (t, c))
-            nc.vector.tensor_tensor(larger[:], fetched[:], st[t][:, lo:hi], ALU.max)
-            larger_of[t, c] = larger
 
         gates = []
         for t in range(PACK):
@@ -133,18 +115,56 @@ def tile_picked_ccmpmaxbtwicp_none_p_kernel(
             for lo, hi in HALVES:
                 nc.scalar.activation(gate[:, lo:hi], y_sb[:].indirect(entries(n1_sb, lo, hi)), ACT.Sigmoid)
             gates.append(gate)
-        for t in range(PACK):
-            st_t = sb.tile([P, S], F32, name="st%d" % t)
-            nc.vector.tensor_tensor(st_t[:], y_ps[t][:], gates[t][:], ALU.mult)
-            st.append(st_t)
-            larger_scaled(t, 0)
+
+        st = [sb.tile([P, S], F32, name="st%d" % t) for t in range(PACK)]
+        larger = [sb.tile([P, S], F32, name="larger%d" % t) for t in range(PACK)]
+
+        def gated(t):
+            nc.vector.tensor_tensor(st[t][:], y_ps[t][:], gates[t][:], ALU.mult)
+
+        def fetch(t, lo, hi, dst):
+            nc.vector.tensor_copy(dst, st[t][:].indirect(entries(n1_sb, lo, hi)))
+
+        def take_larger(t, lo, hi, src):
+            nc.vector.tensor_tensor(larger[t][:, lo:hi], src, st[t][:, lo:hi], ALU.max)
+
+        gated(0)
+        ca_scales = deal_scales("ca_scales", ca_picked, "w_codes0")
+        for t in range(PACK - 1):
+            whole = sb.tile([P, S], F32, name="st_n1_%d" % t)
+            for lo, hi in HALVES:
+                fetch(t, lo, hi, whole[:, lo:hi])
+            gated(t + 1)
+            take_larger(t, 0, S, whole[:])
+        last = PACK - 1
+        parts = [
+            sb.tile([P, hi - lo], F32, name="st_n1_last%d" % c, tag="st_n1_last%d" % c, align_bytes=64)
+            for c, (lo, hi) in enumerate(Z_CHUNKS)
+        ]
+        fetch(last, *Z_CHUNKS[0], parts[0][:])
+        for c in range(len(Z_CHUNKS)):
+            if c + 1 < len(Z_CHUNKS):
+                fetch(last, *Z_CHUNKS[c + 1], parts[c + 1][:])
+            else:
+                cb_picked = pick_scales("cb_picked", cb_sb, "st_n1_last%d" % (c - 1))
+            take_larger(last, *Z_CHUNKS[c], parts[c][:])
+
+        z_rows = [sb.tile([P, PACK, hi - lo], BF16, name="z_rows%d" % c) for c, (lo, hi) in enumerate(Z_CHUNKS)]
+
+        def scale(t, c):
+            lo, hi = Z_CHUNKS[c]
+            nc.scalar.activation(z_rows[c][:, t, :], larger[t][:, lo:hi], ACT.Copy, scale=gs_sb[:, t : t + 1])
+
+        for t in range(PACK - 1):
+            for c in range(len(Z_CHUNKS)):
+                scale(t, c)
 
         z_codes = sb.tile([P, S], U32, name="z_codes", align_bytes=64)
         z_scales = sb.tile([P, S], U8, name="z_scales", align_bytes=64)
 
         def quantize_z(c):
             lo, hi = Z_CHUNKS[c]
-            woven = sb.tile([P, (hi - lo) * PACK], BF16, name="z_woven%d" % c, align_bytes=64)
+            woven = sb.tile([P, (hi - lo) * PACK], BF16, name="z_woven%d" % c, tag="z_woven%d" % c, align_bytes=64)
             nc.scalar.copy(
                 woven[:].rearrange("p (g i t) -> p g t i", i=4, t=PACK),
                 z_rows[c][:].rearrange("p t (g i) -> p g t i", i=4),
@@ -164,15 +184,13 @@ def tile_picked_ccmpmaxbtwicp_none_p_kernel(
             )
             nc.scalar.activation(window[:, lo:hi], bank[:, lo:hi], ACT.Copy, scale=SIXTEENTH)
 
-        for c, (lo, hi) in enumerate(Z_CHUNKS):
-            if c > 0:
-                for t in range(PACK):
-                    larger_scaled(t, c)
-            for t in range(PACK):
-                scale(t, c)
+        for c in range(len(Z_CHUNKS)):
+            scale(last, c)
             quantize_z(c)
+        for lo, hi in Z_CHUNKS:
             score(a_ps[0], a_sb[0], ca_codes, ca_scales, 0, lo, hi)
-        cb_codes = pick_dealt_codes("cb_codes", cb_sb, "st_n1_3_2")
+        cb_codes = pick_dealt_codes("cb_codes", cb_sb, "z_woven0")
+        cb_scales = deal_scales("cb_scales", cb_picked, "z_woven2")
         score(b_ps[0], b_sb[0], cb_codes, cb_scales, 0, 0, S)
         for t in range(1, PACK):
             score(a_ps[t], a_sb[t], ca_codes, ca_scales, t, 0, S)
@@ -185,18 +203,44 @@ def tile_picked_ccmpmaxbtwicp_none_p_kernel(
             upper = sb.tile([P, S], F32, name="upper%d" % t)
             lower = sb.tile([P, S], F32, name="lower%d" % t)
             result = sb.tile([P, S], F32, name="result%d" % t)
-            last = t == PACK - 1
-            for lo, hi in HALVES:
+
+            def fetch_a(lo, hi):
                 nc.vector.tensor_copy(a_n2[:, lo:hi], a_sb[t][:].indirect(entries(n2_sb, lo, hi)))
+
+            def fetch_b(lo, hi):
                 nc.vector.tensor_copy(b_n3[:, lo:hi], b_sb[t][:].indirect(entries(n3_sb, lo, hi)))
-                if last or hi == S:
-                    c0 = lo if last else 0
-                    nc.vector.scalar_tensor_tensor(
-                        lower[:, c0:hi], b_ps[t][:, c0:hi], SIXTEENTH, a_n2[:, c0:hi], ALU.mult, ALU.min
-                    )
-                    nc.vector.scalar_tensor_tensor(
-                        upper[:, c0:hi], a_ps[t][:, c0:hi], SIXTEENTH, b_n3[:, c0:hi], ALU.mult, ALU.max
-                    )
-                    engine = nc.vector if (last and hi == S) else nc.gpsimd
-                    engine.tensor_tensor(result[:, c0:hi], upper[:, c0:hi], lower[:, c0:hi], ALU.subtract)
-                    nc.sync.dma_start(out_rows[:, t, c0:hi], result[:, c0:hi])
+
+            def take_lower(lo, hi):
+                nc.vector.scalar_tensor_tensor(
+                    lower[:, lo:hi], b_ps[t][:, lo:hi], SIXTEENTH, a_n2[:, lo:hi], ALU.mult, ALU.min
+                )
+
+            def take_upper(lo, hi):
+                nc.vector.scalar_tensor_tensor(
+                    upper[:, lo:hi], a_ps[t][:, lo:hi], SIXTEENTH, b_n3[:, lo:hi], ALU.mult, ALU.max
+                )
+
+            def finish(engine, lo, hi):
+                engine.tensor_tensor(result[:, lo:hi], upper[:, lo:hi], lower[:, lo:hi], ALU.subtract)
+                nc.sync.dma_start(out_rows[:, t, lo:hi], result[:, lo:hi])
+
+            first, second = HALVES
+            if t < last:
+                fetch_a(*first)
+                fetch_a(*second)
+                fetch_b(*first)
+                fetch_b(*second)
+                take_lower(0, S)
+                take_upper(0, S)
+                finish(nc.vector, 0, S)
+            else:
+                fetch_b(*first)
+                fetch_a(*first)
+                fetch_b(*second)
+                take_upper(*first)
+                take_lower(*first)
+                finish(nc.vector, *first)
+                fetch_a(*second)
+                take_upper(*second)
+                take_lower(*second)
+                finish(nc.vector, *second)

@@ -21,6 +21,7 @@ LANES = 16
 HALVES = ((0, 256), (256, 512))
 Z_CHUNKS = ((0, 256), (256, 384), (384, 512))
 SIXTEENTH = 0.0625
+RELU_TILES = 2
 
 
 def tile_picked_ccmpmaxbtwicp_none_p_kernel(
@@ -40,31 +41,36 @@ def tile_picked_ccmpmaxbtwicp_none_p_kernel(
         def entries(tile, lo, hi):
             return tile[:, lo // LANES : hi // LANES]
 
+        w_rows = w1.rearrange("(p j) c -> p j c", j=PACK)
+
+        def load_w(h):
+            lo, hi = HALVES[h]
+            raw = sb.tile([P, PACK, hi - lo], F32, name="w_raw%d" % h)
+            nc.sync.dma_start(raw[:], w_rows[:, :, lo:hi])
+            return raw
+
+        offs_sb = load_list("offs_sb", offs)
+        w_raw = [load_w(0)]
         x_plane = sb.tile([P, T], U8, name="x_plane", align_bytes=64)
-        nc.vector.memset(x_plane[:].bitcast(I32), 0)
+        nc.gpsimd.memset(x_plane[:, : T // 2].bitcast(I32), 0)
+        nc.vector.memset(x_plane[:, T // 2 :].bitcast(I32), 0)
         for q in range(4):
-            nc.scalar.dma_start(
+            (nc.sync if q % 2 else nc.scalar).dma_start(
                 x_plane[32 * q : 32 * q + 4, :].bitcast(I32), x_scales[0, 4 * q : 4 * q + 4, :].bitcast(I32)
             )
         warm = sb.tile([P, 8], F32, name="warm")
         nc.vector.memset(warm[:], 0.0)
         nc.scalar.activation(warm[:, 1:2], warm[:, 0:1], ACT.Sigmoid)
-        offs_sb = load_list("offs_sb", offs)
+        w_raw.append(load_w(1))
+        ca_sb = load_list("ca_sb", ca)
         x_codes = sb.tile([P, T], U32, name="x_codes", align_bytes=64)
         nc.sync.dma_start(x_codes[:].bitcast(I32), x_words[0].rearrange("p n t -> p (n t)").bitcast(I32))
-        ca_sb = load_list("ca_sb", ca)
-        w_rows = w1.rearrange("(p j) c -> p j c", j=PACK)
-        w_raw = []
-        for h, (lo, hi) in enumerate(HALVES):
-            raw = sb.tile([P, PACK, hi - lo], F32, name="w_raw%d" % h, tag="w_raw%d" % h, align_bytes=64)
-            nc.sync.dma_start(raw[:], w_rows[:, :, lo:hi])
-            w_raw.append(raw)
-        cb_sb = load_list("cb_sb", cb)
         n1_sb = load_list("n1_sb", n1)
+        cb_sb = load_list("cb_sb", cb)
         gs_sb = sb.tile([P, PACK], F32, name="gs_sb")
         nc.sync.dma_start(gs_sb[:], gs.rearrange("(p t) one -> p (t one)", t=PACK))
-        n3_sb = load_list("n3_sb", n3)
         n2_sb = load_list("n2_sb", n2)
+        n3_sb = load_list("n3_sb", n3)
 
         def pick_scales(name, list_sb, tag):
             picked = sb.tile([P, S], U8, name=name, tag=tag, align_bytes=64)
@@ -83,44 +89,67 @@ def tile_picked_ccmpmaxbtwicp_none_p_kernel(
             nc.vector.tensor_copy(dealt[:].rearrange("p (t m) -> p m t", t=PACK), x_codes[:].indirect(list_sb[:]))
             return dealt
 
-        xq_codes = sb.tile([P, S], U32, name="xq_codes", align_bytes=64)
-        nc.vector.tensor_copy(xq_codes[:], x_codes[:].indirect(offs_sb[:]))
         xq_scales = pick_scales("xq_scales", offs_sb, "xq_scales")
         ca_picked = pick_scales("ca_picked", ca_sb, "ca_picked")
 
-        w_bf = sb.tile([P, PACK, P, PACK], BF16, name="w_bf", tag="w_bf", align_bytes=64)
+        w_bf = [
+            sb.tile([P, 2, P, PACK], BF16, name="w_bf%d" % u, tag="w_bf%d" % u, align_bytes=64) for u in range(2)
+        ]
         for h, (lo, hi) in enumerate(HALVES):
-            src = w_raw[h][:].rearrange("p j (m t) -> p m t j", t=PACK)
-            dst = w_bf[:, :, lo // PACK : hi // PACK, :].rearrange("p t m j -> p m t j")
-            nc.scalar.copy(dst, src)
-        y_ps = []
+            for u in range(2):
+                src = w_raw[h][:].rearrange("p j (m t) -> p m j t", t=PACK)[:, :, :, 2 * u : 2 * u + 2]
+                dst = w_bf[u][:, :, lo // PACK : hi // PACK, :].rearrange("p t m j -> p m j t")
+                nc.scalar.copy(dst, src)
+        w_mx = []
         for t in range(PACK):
             w_codes = sb.tile([P, P], U32, name="w_codes%d" % t, tag="w_codes%d" % t, align_bytes=64)
             w_scales = sb.tile([P, P], U8, name="w_scales%d" % t, align_bytes=64)
-            nc.vector.quantize_mx(w_codes[:].bitcast(FP8X4), w_scales[:], w_bf[:, t].rearrange("p m j -> p (m j)"))
-            bank = psum.tile([P, S], F32, name="y_ps%d" % t, tag="bank%d" % (4 + t))
-            nc.tensor.matmul_mx(
-                bank[:], w_codes[:].bitcast(FP8X4), w_scales[:],
-                xq_codes[:].bitcast(FP8X4), xq_scales[:], start=True, stop=True,
+            nc.vector.quantize_mx(
+                w_codes[:].bitcast(FP8X4), w_scales[:], w_bf[t // 2][:, t % 2].rearrange("p m j -> p (m j)")
             )
-            y_ps.append(bank)
+            w_mx.append((w_codes, w_scales))
+        xq_codes = []
+        for h, (lo, hi) in enumerate(HALVES):
+            half = sb.tile([P, hi - lo], U32, name="xq_codes%d" % h, align_bytes=64)
+            nc.vector.tensor_copy(half[:], x_codes[:].indirect(entries(offs_sb, lo, hi)))
+            xq_codes.append(half)
+        y_sb = [sb.tile([P, S], F32, name="y_sb%d" % t) for t in range(PACK)]
+        y_banks = [(0, lo, hi) for lo, hi in HALVES] + [(t, 0, S) for t in range(1, PACK)]
+        y_banks = [
+            (t, lo, hi, psum.tile([P, hi - lo], F32, name="y_ps%d" % n, tag="bank%d" % n))
+            for n, (t, lo, hi) in enumerate(y_banks)
+        ]
+        for t, start, stop, bank in y_banks:
+            w_codes, w_scales = w_mx[t]
+            for h, (lo, hi) in enumerate(HALVES):
+                if start <= lo and hi <= stop:
+                    nc.tensor.matmul_mx(
+                        bank[:, lo - start : hi - start], w_codes[:].bitcast(FP8X4), w_scales[:],
+                        xq_codes[h][:].bitcast(FP8X4), xq_scales[:, lo:hi], start=True, stop=True,
+                    )
 
-        ca_codes = pick_dealt_codes("ca_codes", ca_sb, "w_bf")
-
-        gates = []
-        for t in range(PACK):
-            y_sb = sb.tile([P, S], F32, name="y_sb%d" % t)
-            nc.scalar.copy(y_sb[:], y_ps[t][:])
-            gate = sb.tile([P, S], F32, name="gate%d" % t)
-            for lo, hi in HALVES:
-                nc.scalar.activation(gate[:, lo:hi], y_sb[:].indirect(entries(n1_sb, lo, hi)), ACT.Sigmoid)
-            gates.append(gate)
+        ca_codes = pick_dealt_codes("ca_codes", ca_sb, "ca_codes")
+        ca_scales = deal_scales("ca_scales", ca_picked, "w_codes0")
+        cb_picked = pick_scales("cb_picked", cb_sb, "w_codes1")
+        cb_scales = deal_scales("cb_scales", cb_picked, "cb_scales")
 
         st = [sb.tile([P, S], F32, name="st%d" % t) for t in range(PACK)]
-        larger = [sb.tile([P, S], F32, name="larger%d" % t) for t in range(PACK)]
 
-        def gated(t):
-            nc.vector.tensor_tensor(st[t][:], y_ps[t][:], gates[t][:], ALU.mult)
+        def y_to_window(t):
+            for bank_t, lo, hi, bank in y_banks:
+                if bank_t == t:
+                    nc.scalar.copy(y_sb[t][:, lo:hi], bank[:])
+
+        y_to_window(0)
+        for t in range(PACK):
+            gate = sb.tile([P, S], F32, name="gate%d" % t)
+            for lo, hi in HALVES:
+                nc.scalar.activation(gate[:, lo:hi], y_sb[t][:].indirect(entries(n1_sb, lo, hi)), ACT.Sigmoid)
+                nc.gpsimd.tensor_tensor(st[t][:, lo:hi], y_sb[t][:, lo:hi], gate[:, lo:hi], ALU.mult)
+                if lo == 0 and t + 1 < PACK:
+                    y_to_window(t + 1)
+
+        larger = [sb.tile([P, S], F32, name="larger%d" % t) for t in range(PACK)]
 
         def fetch(t, lo, hi, dst):
             nc.vector.tensor_copy(dst, st[t][:].indirect(entries(n1_sb, lo, hi)))
@@ -128,119 +157,166 @@ def tile_picked_ccmpmaxbtwicp_none_p_kernel(
         def take_larger(t, lo, hi, src):
             nc.vector.tensor_tensor(larger[t][:, lo:hi], src, st[t][:, lo:hi], ALU.max)
 
-        gated(0)
-        ca_scales = deal_scales("ca_scales", ca_picked, "w_codes0")
         for t in range(PACK - 1):
             whole = sb.tile([P, S], F32, name="st_n1_%d" % t)
             for lo, hi in HALVES:
                 fetch(t, lo, hi, whole[:, lo:hi])
-            gated(t + 1)
-            take_larger(t, 0, S, whole[:])
+            for lo, hi in HALVES:
+                take_larger(t, lo, hi, whole[:, lo:hi])
         last = PACK - 1
-        parts = [
-            sb.tile([P, hi - lo], F32, name="st_n1_last%d" % c, tag="st_n1_last%d" % c, align_bytes=64)
-            for c, (lo, hi) in enumerate(Z_CHUNKS)
-        ]
-        fetch(last, *Z_CHUNKS[0], parts[0][:])
-        for c in range(len(Z_CHUNKS)):
-            if c + 1 < len(Z_CHUNKS):
-                fetch(last, *Z_CHUNKS[c + 1], parts[c + 1][:])
-            else:
-                cb_picked = pick_scales("cb_picked", cb_sb, "st_n1_last%d" % (c - 1))
-            take_larger(last, *Z_CHUNKS[c], parts[c][:])
+        z_rows = sb.tile([P, S // P, PACK, P], BF16, name="z_rows")
 
-        z_rows = [sb.tile([P, PACK, hi - lo], BF16, name="z_rows%d" % c) for c, (lo, hi) in enumerate(Z_CHUNKS)]
+        def z_rows_of(t, lo, hi):
+            return z_rows[:, lo // P : hi // P, t, :]
 
-        def scale(t, c):
-            lo, hi = Z_CHUNKS[c]
-            nc.scalar.activation(z_rows[c][:, t, :], larger[t][:, lo:hi], ACT.Copy, scale=gs_sb[:, t : t + 1])
+        def larger_of(t, lo, hi):
+            return larger[t][:, lo:hi].rearrange("p (c i) -> p c i", i=P)
 
-        for t in range(PACK - 1):
-            for c in range(len(Z_CHUNKS)):
-                scale(t, c)
+        for t in range(last):
+            nc.scalar.activation(z_rows_of(t, 0, S), larger_of(t, 0, S), ACT.Copy, scale=gs_sb[:, t : t + 1])
+
+        def scale_last(lo, hi):
+            nc.vector.tensor_scalar(
+                z_rows_of(last, lo, hi), larger_of(last, lo, hi), gs_sb[:, last : last + 1], None, ALU.mult
+            )
 
         z_codes = sb.tile([P, S], U32, name="z_codes", align_bytes=64)
         z_scales = sb.tile([P, S], U8, name="z_scales", align_bytes=64)
+        woven = [
+            sb.tile([P, 2, P * PACK], BF16, name="z_woven%d" % h, tag="z_woven%d" % h, align_bytes=64) for h in range(2)
+        ]
 
-        def quantize_z(c):
-            lo, hi = Z_CHUNKS[c]
-            woven = sb.tile([P, (hi - lo) * PACK], BF16, name="z_woven%d" % c, tag="z_woven%d" % c, align_bytes=64)
-            nc.scalar.copy(
-                woven[:].rearrange("p (g i t) -> p g t i", i=4, t=PACK),
-                z_rows[c][:].rearrange("p t (g i) -> p g t i", i=4),
+        def weave(copy, block):
+            copy(
+                woven[block // 2][:, block % 2].rearrange("p (g i t) -> p g t i", i=4, t=PACK),
+                z_rows[:, block].rearrange("p t (g i) -> p g t i", i=4),
             )
-            nc.vector.quantize_mx(z_codes[:, lo:hi].bitcast(FP8X4), z_scales[:, lo:hi], woven[:])
 
-        a_ps = [psum.tile([P, S], F32, name="a_ps%d" % t, tag="bank%d" % (2 * t)) for t in range(PACK)]
-        b_ps = [psum.tile([P, S], F32, name="b_ps%d" % t, tag="bank%d" % (2 * t + 1)) for t in range(PACK)]
+        def quantize_z(h):
+            lo, hi = HALVES[h]
+            nc.vector.quantize_mx(
+                z_codes[:, lo:hi].bitcast(FP8X4), z_scales[:, lo:hi], woven[h][:].rearrange("p b w -> p (b w)")
+            )
+
+        st_n1 = sb.tile([P, S], F32, name="st_n1_last")
+        head, third, fourth = Z_CHUNKS
+        fetch(last, *head, st_n1[:, slice(*head)])
+        fetch(last, *third, st_n1[:, slice(*third)])
+        take_larger(last, *head, st_n1[:, slice(*head)])
+        fetch(last, *fourth, st_n1[:, slice(*fourth)])
+        scale_last(*head)
+        take_larger(last, *third, st_n1[:, slice(*third)])
+        take_larger(last, *fourth, st_n1[:, slice(*fourth)])
+        weave(nc.scalar.copy, 0)
+        weave(nc.vector.tensor_copy, 1)
+        scale_last(third[0], fourth[1])
+        quantize_z(0)
+        weave(nc.scalar.copy, 2)
+        weave(nc.vector.tensor_copy, 3)
+        quantize_z(1)
+
         a_sb = [sb.tile([P, S], F32, name="a_sb%d" % t) for t in range(PACK)]
         b_sb = [sb.tile([P, S], F32, name="b_sb%d" % t) for t in range(PACK)]
 
-        def score(bank, window, codes, scales, t, lo, hi):
+        def score(dst, codes, scales, t, lo, hi):
             cols = slice(t * P, (t + 1) * P)
             nc.tensor.matmul_mx(
-                bank[:, lo:hi], codes[:, cols].bitcast(FP8X4), scales[:, cols],
+                dst, codes[:, cols].bitcast(FP8X4), scales[:, cols],
                 z_codes[:, lo:hi].bitcast(FP8X4), z_scales[:, lo:hi], start=True, stop=True,
             )
-            nc.scalar.activation(window[:, lo:hi], bank[:, lo:hi], ACT.Copy, scale=SIXTEENTH)
 
-        for c in range(len(Z_CHUNKS)):
-            scale(last, c)
-            quantize_z(c)
-        for lo, hi in Z_CHUNKS:
-            score(a_ps[0], a_sb[0], ca_codes, ca_scales, 0, lo, hi)
-        cb_codes = pick_dealt_codes("cb_codes", cb_sb, "z_woven0")
-        cb_scales = deal_scales("cb_scales", cb_picked, "z_woven2")
-        score(b_ps[0], b_sb[0], cb_codes, cb_scales, 0, 0, S)
-        for t in range(1, PACK):
-            score(a_ps[t], a_sb[t], ca_codes, ca_scales, t, 0, S)
-            score(b_ps[t], b_sb[t], cb_codes, cb_scales, t, 0, S)
+        def to_window(dst, src):
+            nc.scalar.activation(dst, src, ACT.Copy, scale=SIXTEENTH)
+
+        a_ps = [[]]
+        for h, (lo, hi) in enumerate(HALVES):
+            bank = psum.tile([P, hi - lo], F32, name="a_ps0_%d" % h, tag="bank%d" % (5 + h))
+            score(bank[:], ca_codes, ca_scales, 0, lo, hi)
+            to_window(a_sb[0][:, lo:hi], bank[:])
+            a_ps[0].append((lo, hi, bank))
+        b_ps = []
+
+        def score_a(t, tag):
+            bank = psum.tile([P, S], F32, name="a_ps%d" % t, tag=tag)
+            score(bank[:], ca_codes, ca_scales, t, 0, S)
+            to_window(a_sb[t][:], bank[:])
+            a_ps.append([(0, S, bank)])
+
+        def score_b(t, tag):
+            bank = psum.tile([P, S], F32, name="b_ps%d" % t, tag=tag)
+            score(bank[:], cb_codes, cb_scales, t, 0, S)
+            to_window(b_sb[t][:], bank[:])
+            b_ps.append(bank)
 
         out_rows = out.rearrange("(p t) j -> p t j", t=PACK)
-        for t in range(PACK):
-            a_n2 = sb.tile([P, S], F32, name="a_n2_%d" % t)
-            b_n3 = sb.tile([P, S], F32, name="b_n3_%d" % t)
-            upper = sb.tile([P, S], F32, name="upper%d" % t)
-            lower = sb.tile([P, S], F32, name="lower%d" % t)
-            result = sb.tile([P, S], F32, name="result%d" % t)
+        a_n2 = [sb.tile([P, S], F32, name="a_n2_%d" % t) for t in range(PACK)]
+        b_n3 = [sb.tile([P, S], F32, name="b_n3_%d" % t) for t in range(PACK)]
+        upper = [sb.tile([P, S], F32, name="upper%d" % t) for t in range(PACK)]
+        lower = {t: sb.tile([P, S], F32, name="lower%d" % t, tag="lower%d" % t) for t in (2, 3)}
 
-            def fetch_a(lo, hi):
-                nc.vector.tensor_copy(a_n2[:, lo:hi], a_sb[t][:].indirect(entries(n2_sb, lo, hi)))
+        def fetch_a(t, lo, hi):
+            nc.vector.tensor_copy(a_n2[t][:, lo:hi], a_sb[t][:].indirect(entries(n2_sb, lo, hi)))
 
-            def fetch_b(lo, hi):
-                nc.vector.tensor_copy(b_n3[:, lo:hi], b_sb[t][:].indirect(entries(n3_sb, lo, hi)))
+        def fetch_b(t, lo, hi):
+            nc.vector.tensor_copy(b_n3[t][:, lo:hi], b_sb[t][:].indirect(entries(n3_sb, lo, hi)))
 
-            def take_lower(lo, hi):
+        def take_lower(t, lo, hi):
+            nc.vector.scalar_tensor_tensor(
+                lower[t][:, lo:hi], b_ps[t][:, lo:hi], SIXTEENTH, a_n2[t][:, lo:hi], ALU.mult, ALU.min
+            )
+
+        def take_upper(t, lo, hi):
+            for start, stop, bank in a_ps[t]:
+                c0, c1 = max(lo, start), min(hi, stop)
                 nc.vector.scalar_tensor_tensor(
-                    lower[:, lo:hi], b_ps[t][:, lo:hi], SIXTEENTH, a_n2[:, lo:hi], ALU.mult, ALU.min
+                    upper[t][:, c0:c1], bank[:, c0 - start : c1 - start], SIXTEENTH, b_n3[t][:, c0:c1], ALU.mult, ALU.max
                 )
 
-            def take_upper(lo, hi):
-                nc.vector.scalar_tensor_tensor(
-                    upper[:, lo:hi], a_ps[t][:, lo:hi], SIXTEENTH, b_n3[:, lo:hi], ALU.mult, ALU.max
-                )
+        def finish(engine, op, in0, in1, tag, t, lo, hi):
+            result = sb.tile([P, hi - lo], F32, name="result%d_%d" % (t, lo), tag=tag)
+            engine.tensor_tensor(result[:], in0[:, lo:hi], in1[:, lo:hi], op)
+            nc.sync.dma_start(out_rows[:, t, lo:hi], result[:])
 
-            def finish(engine, lo, hi):
-                engine.tensor_tensor(result[:, lo:hi], upper[:, lo:hi], lower[:, lo:hi], ALU.subtract)
-                nc.sync.dma_start(out_rows[:, t, lo:hi], result[:, lo:hi])
+        score_a(1, "bank0")
+        cb_codes = pick_dealt_codes("cb_codes", cb_sb, "z_woven1")
+        score_b(0, "bank7")
+        score_b(1, "bank1")
+        for t in range(2):
+            for lo, hi in HALVES:
+                fetch_a(t, lo, hi)
+        excess = []
+        for t in range(2):
+            gap = sb.tile([P, S], F32, name="gap%d" % t)
+            nc.gpsimd.tensor_tensor(gap[:], a_n2[t][:], b_sb[t][:], ALU.subtract)
+            above = sb.tile([P, S], F32, name="excess%d" % t)
+            nc.scalar.activation(above[:], gap[:], ACT.Relu)
+            excess.append(above)
+        for t in range(2):
+            for lo, hi in HALVES:
+                fetch_b(t, lo, hi)
+            take_upper(t, 0, S)
+            rest = sb.tile([P, S], F32, name="rest%d" % t, tag="rest%d" % t)
+            nc.gpsimd.tensor_tensor(rest[:], upper[t][:], a_n2[t][:], ALU.subtract)
+            finish(nc.gpsimd, ALU.add, rest, excess[t], "result%d" % t, t, 0, S)
+            score_a(t + 2, ("bank7", "bank1")[t])
+            score_b(t + 2, ("bank2", "bank3")[t])
 
-            first, second = HALVES
-            if t < last:
-                fetch_a(*first)
-                fetch_a(*second)
-                fetch_b(*first)
-                fetch_b(*second)
-                take_lower(0, S)
-                take_upper(0, S)
-                finish(nc.vector, 0, S)
-            else:
-                fetch_b(*first)
-                fetch_a(*first)
-                fetch_b(*second)
-                take_upper(*first)
-                take_lower(*first)
-                finish(nc.vector, *first)
-                fetch_a(*second)
-                take_upper(*second)
-                take_lower(*second)
-                finish(nc.vector, *second)
+        first, second = HALVES
+        for lo, hi in HALVES:
+            fetch_a(2, lo, hi)
+        for lo, hi in HALVES:
+            fetch_b(2, lo, hi)
+        take_lower(2, 0, S)
+        take_upper(2, 0, S)
+        finish(nc.gpsimd, ALU.subtract, upper[2], lower[2], "rest1", 2, 0, S)
+
+        fetch_b(last, *first)
+        fetch_a(last, *first)
+        fetch_b(last, *second)
+        take_upper(last, *first)
+        take_lower(last, *first)
+        finish(nc.gpsimd, ALU.subtract, upper[last], lower[last], "lower2", last, *first)
+        fetch_a(last, *second)
+        take_upper(last, *second)
+        take_lower(last, *second)
+        finish(nc.vector, ALU.subtract, upper[last], lower[last], "result_last", last, *second)

@@ -2,8 +2,8 @@ from contextlib import ExitStack
 
 import concourse.mybir as mybir
 
-K, T, S, H, C = 512, 2048, 512, 512, 512
-FLOPS = 3 * 2 * 512 * 512 * 512
+K, T, S = 512, 2048, 512
+FLOPS = 3 * 2 * K * S * S
 
 F32 = mybir.dt.float32
 BF16 = mybir.dt.bfloat16
@@ -17,11 +17,10 @@ ACT = mybir.ActivationFunctionType
 
 P = 128
 PACK = 4
-LANES = 16
-HALVES = ((0, 256), (256, 512))
-Z_CHUNKS = ((0, 256), (256, 384), (384, 512))
+LAST = PACK - 1
+GROUP = 16
+FIRST, SECOND = HALVES = ((0, S // 2), (S // 2, S))
 SIXTEENTH = 0.0625
-RELU_TILES = 2
 
 
 def tile_picked_ccmpmaxbtwicp_none_p_kernel(
@@ -34,19 +33,17 @@ def tile_picked_ccmpmaxbtwicp_none_p_kernel(
         psum = ctx.enter_context(tc.psum_pool(name="psum", bufs=1))
 
         def load_list(name, src):
-            tile = lists.tile([P, S // LANES], U16, name=name)
-            nc.sync.dma_start(tile[:], src)
-            return tile
+            list_sb = lists.tile([P, S // GROUP], U16, name=name)
+            nc.sync.dma_start(list_sb[:], src)
+            return list_sb
 
-        def entries(tile, lo, hi):
-            return tile[:, lo // LANES : hi // LANES]
-
-        w_rows = w1.rearrange("(p j) c -> p j c", j=PACK)
+        def entries(list_sb, lo, hi):
+            return list_sb[:, lo // GROUP : hi // GROUP]
 
         def load_w(h):
             lo, hi = HALVES[h]
             raw = sb.tile([P, PACK, hi - lo], F32, name="w_raw%d" % h)
-            nc.sync.dma_start(raw[:], w_rows[:, :, lo:hi])
+            nc.sync.dma_start(raw[:], w1.rearrange("(p j) c -> p j c", j=PACK)[:, :, lo:hi])
             return raw
 
         offs_sb = load_list("offs_sb", offs)
@@ -58,8 +55,8 @@ def tile_picked_ccmpmaxbtwicp_none_p_kernel(
             (nc.sync if q % 2 else nc.scalar).dma_start(
                 x_plane[32 * q : 32 * q + 4, :].bitcast(I32), x_scales[0, 4 * q : 4 * q + 4, :].bitcast(I32)
             )
-        warm = sb.tile([P, 8], F32, name="warm")
-        nc.vector.memset(warm[:], 0.0)
+        warm = sb.tile([P, 2], F32, name="warm")
+        nc.vector.memset(warm[:, 0:1], 0.0)
         nc.scalar.activation(warm[:, 1:2], warm[:, 0:1], ACT.Sigmoid)
         w_raw.append(load_w(1))
         ca_sb = load_list("ca_sb", ca)
@@ -92,14 +89,13 @@ def tile_picked_ccmpmaxbtwicp_none_p_kernel(
         xq_scales = pick_scales("xq_scales", offs_sb, "xq_scales")
         ca_picked = pick_scales("ca_picked", ca_sb, "ca_picked")
 
-        w_bf = [
-            sb.tile([P, 2, P, PACK], BF16, name="w_bf%d" % u, tag="w_bf%d" % u, align_bytes=64) for u in range(2)
-        ]
+        w_bf = [sb.tile([P, 2, P, PACK], BF16, name="w_bf%d" % u, align_bytes=64) for u in range(2)]
         for h, (lo, hi) in enumerate(HALVES):
             for u in range(2):
-                src = w_raw[h][:].rearrange("p j (m t) -> p m j t", t=PACK)[:, :, :, 2 * u : 2 * u + 2]
-                dst = w_bf[u][:, :, lo // PACK : hi // PACK, :].rearrange("p t m j -> p m j t")
-                nc.scalar.copy(dst, src)
+                nc.scalar.copy(
+                    w_bf[u][:, :, lo // PACK : hi // PACK, :].rearrange("p t m j -> p m j t"),
+                    w_raw[h][:].rearrange("p j (m t) -> p m j t", t=PACK)[:, :, :, 2 * u : 2 * u + 2],
+                )
         w_mx = []
         for t in range(PACK):
             w_codes = sb.tile([P, P], U32, name="w_codes%d" % t, tag="w_codes%d" % t, align_bytes=64)
@@ -108,18 +104,16 @@ def tile_picked_ccmpmaxbtwicp_none_p_kernel(
                 w_codes[:].bitcast(FP8X4), w_scales[:], w_bf[t // 2][:, t % 2].rearrange("p m j -> p (m j)")
             )
             w_mx.append((w_codes, w_scales))
+
         xq_codes = []
         for h, (lo, hi) in enumerate(HALVES):
             half = sb.tile([P, hi - lo], U32, name="xq_codes%d" % h, align_bytes=64)
             nc.vector.tensor_copy(half[:], x_codes[:].indirect(entries(offs_sb, lo, hi)))
             xq_codes.append(half)
         y_sb = [sb.tile([P, S], F32, name="y_sb%d" % t) for t in range(PACK)]
-        y_banks = [(0, lo, hi) for lo, hi in HALVES] + [(t, 0, S) for t in range(1, PACK)]
-        y_banks = [
-            (t, lo, hi, psum.tile([P, hi - lo], F32, name="y_ps%d" % n, tag="bank%d" % n))
-            for n, (t, lo, hi) in enumerate(y_banks)
-        ]
-        for t, start, stop, bank in y_banks:
+
+        def project(tag, t, start, stop):
+            bank = psum.tile([P, stop - start], F32, name="y_ps%d_%d" % (t, start), tag=tag)
             w_codes, w_scales = w_mx[t]
             for h, (lo, hi) in enumerate(HALVES):
                 if start <= lo and hi <= stop:
@@ -127,44 +121,38 @@ def tile_picked_ccmpmaxbtwicp_none_p_kernel(
                         bank[:, lo - start : hi - start], w_codes[:].bitcast(FP8X4), w_scales[:],
                         xq_codes[h][:].bitcast(FP8X4), xq_scales[:, lo:hi], start=True, stop=True,
                     )
+            return bank
+
+        y0_banks = [project("bank0", 0, *FIRST), project("bank1", 0, *SECOND)]
+        y1_bank = project("bank2", 1, 0, S)
+        for (lo, hi), bank in zip(HALVES, y0_banks):
+            nc.scalar.copy(y_sb[0][:, lo:hi], bank[:])
 
         ca_codes = pick_dealt_codes("ca_codes", ca_sb, "ca_codes")
+        nc.vector.tensor_copy(y_sb[1][:], y1_bank[:])
         ca_scales = deal_scales("ca_scales", ca_picked, "w_codes0")
         cb_picked = pick_scales("cb_picked", cb_sb, "w_codes1")
         cb_scales = deal_scales("cb_scales", cb_picked, "cb_scales")
+        later_banks = {2: project("bank1", 2, 0, S), 3: project("bank2", 3, 0, S)}
 
         st = [sb.tile([P, S], F32, name="st%d" % t) for t in range(PACK)]
-
-        def y_to_window(t):
-            for bank_t, lo, hi, bank in y_banks:
-                if bank_t == t:
-                    nc.scalar.copy(y_sb[t][:, lo:hi], bank[:])
-
-        y_to_window(0)
         for t in range(PACK):
             gate = sb.tile([P, S], F32, name="gate%d" % t)
             for lo, hi in HALVES:
                 nc.scalar.activation(gate[:, lo:hi], y_sb[t][:].indirect(entries(n1_sb, lo, hi)), ACT.Sigmoid)
                 nc.gpsimd.tensor_tensor(st[t][:, lo:hi], y_sb[t][:, lo:hi], gate[:, lo:hi], ALU.mult)
-                if lo == 0 and t + 1 < PACK:
-                    y_to_window(t + 1)
+                if lo == 0 and t + 1 in later_banks:
+                    nc.scalar.copy(y_sb[t + 1][:], later_banks[t + 1][:])
 
+        st_n1 = [sb.tile([P, S], F32, name="st_n1_%d" % t) for t in range(PACK)]
         larger = [sb.tile([P, S], F32, name="larger%d" % t) for t in range(PACK)]
-
-        def fetch(t, lo, hi, dst):
-            nc.vector.tensor_copy(dst, st[t][:].indirect(entries(n1_sb, lo, hi)))
-
-        def take_larger(t, lo, hi, src):
-            nc.vector.tensor_tensor(larger[t][:, lo:hi], src, st[t][:, lo:hi], ALU.max)
-
-        for t in range(PACK - 1):
-            whole = sb.tile([P, S], F32, name="st_n1_%d" % t)
-            for lo, hi in HALVES:
-                fetch(t, lo, hi, whole[:, lo:hi])
-            for lo, hi in HALVES:
-                take_larger(t, lo, hi, whole[:, lo:hi])
-        last = PACK - 1
         z_rows = sb.tile([P, S // P, PACK, P], BF16, name="z_rows")
+
+        def fetch_st(t, lo, hi):
+            nc.vector.tensor_copy(st_n1[t][:, lo:hi], st[t][:].indirect(entries(n1_sb, lo, hi)))
+
+        def take_larger(t, lo, hi):
+            nc.vector.tensor_tensor(larger[t][:, lo:hi], st_n1[t][:, lo:hi], st[t][:, lo:hi], ALU.max)
 
         def z_rows_of(t, lo, hi):
             return z_rows[:, lo // P : hi // P, t, :]
@@ -172,12 +160,17 @@ def tile_picked_ccmpmaxbtwicp_none_p_kernel(
         def larger_of(t, lo, hi):
             return larger[t][:, lo:hi].rearrange("p (c i) -> p c i", i=P)
 
-        for t in range(last):
+        for t in range(LAST):
+            for lo, hi in HALVES:
+                fetch_st(t, lo, hi)
+            for lo, hi in HALVES:
+                take_larger(t, lo, hi)
+        for t in range(LAST):
             nc.scalar.activation(z_rows_of(t, 0, S), larger_of(t, 0, S), ACT.Copy, scale=gs_sb[:, t : t + 1])
 
         def scale_last(lo, hi):
             nc.vector.tensor_scalar(
-                z_rows_of(last, lo, hi), larger_of(last, lo, hi), gs_sb[:, last : last + 1], None, ALU.mult
+                z_rows_of(LAST, lo, hi), larger_of(LAST, lo, hi), gs_sb[:, LAST : LAST + 1], None, ALU.mult
             )
 
         z_codes = sb.tile([P, S], U32, name="z_codes", align_bytes=64)
@@ -198,18 +191,17 @@ def tile_picked_ccmpmaxbtwicp_none_p_kernel(
                 z_codes[:, lo:hi].bitcast(FP8X4), z_scales[:, lo:hi], woven[h][:].rearrange("p b w -> p (b w)")
             )
 
-        st_n1 = sb.tile([P, S], F32, name="st_n1_last")
-        head, third, fourth = Z_CHUNKS
-        fetch(last, *head, st_n1[:, slice(*head)])
-        fetch(last, *third, st_n1[:, slice(*third)])
-        take_larger(last, *head, st_n1[:, slice(*head)])
-        fetch(last, *fourth, st_n1[:, slice(*fourth)])
-        scale_last(*head)
-        take_larger(last, *third, st_n1[:, slice(*third)])
-        take_larger(last, *fourth, st_n1[:, slice(*fourth)])
+        third, fourth = (S // 2, 3 * S // 4), (3 * S // 4, S)
+        fetch_st(LAST, *FIRST)
+        fetch_st(LAST, *third)
+        take_larger(LAST, *FIRST)
+        fetch_st(LAST, *fourth)
+        scale_last(*FIRST)
+        take_larger(LAST, *third)
+        take_larger(LAST, *fourth)
         weave(nc.scalar.copy, 0)
         weave(nc.vector.tensor_copy, 1)
-        scale_last(third[0], fourth[1])
+        scale_last(*SECOND)
         quantize_z(0)
         weave(nc.scalar.copy, 2)
         weave(nc.vector.tensor_copy, 3)
@@ -217,36 +209,32 @@ def tile_picked_ccmpmaxbtwicp_none_p_kernel(
 
         a_sb = [sb.tile([P, S], F32, name="a_sb%d" % t) for t in range(PACK)]
         b_sb = [sb.tile([P, S], F32, name="b_sb%d" % t) for t in range(PACK)]
+        a_banks = [[] for t in range(PACK)]
+        b_bank = {}
 
-        def score(dst, codes, scales, t, lo, hi):
+        def score(name, tag, window, codes, scales, t, lo, hi):
             cols = slice(t * P, (t + 1) * P)
+            bank = psum.tile([P, hi - lo], F32, name=name, tag=tag)
             nc.tensor.matmul_mx(
-                dst, codes[:, cols].bitcast(FP8X4), scales[:, cols],
+                bank[:], codes[:, cols].bitcast(FP8X4), scales[:, cols],
                 z_codes[:, lo:hi].bitcast(FP8X4), z_scales[:, lo:hi], start=True, stop=True,
             )
+            nc.scalar.activation(window[:, lo:hi], bank[:], ACT.Copy, scale=SIXTEENTH)
+            return bank
 
-        def to_window(dst, src):
-            nc.scalar.activation(dst, src, ACT.Copy, scale=SIXTEENTH)
-
-        a_ps = [[]]
-        for h, (lo, hi) in enumerate(HALVES):
-            bank = psum.tile([P, hi - lo], F32, name="a_ps0_%d" % h, tag="bank%d" % (5 + h))
-            score(bank[:], ca_codes, ca_scales, 0, lo, hi)
-            to_window(a_sb[0][:, lo:hi], bank[:])
-            a_ps[0].append((lo, hi, bank))
-        b_ps = []
-
-        def score_a(t, tag):
-            bank = psum.tile([P, S], F32, name="a_ps%d" % t, tag=tag)
-            score(bank[:], ca_codes, ca_scales, t, 0, S)
-            to_window(a_sb[t][:], bank[:])
-            a_ps.append([(0, S, bank)])
+        def score_a(t, tag, lo, hi):
+            bank = score("a_ps%d_%d" % (t, lo), tag, a_sb[t], ca_codes, ca_scales, t, lo, hi)
+            a_banks[t].append((lo, hi, bank))
 
         def score_b(t, tag):
-            bank = psum.tile([P, S], F32, name="b_ps%d" % t, tag=tag)
-            score(bank[:], cb_codes, cb_scales, t, 0, S)
-            to_window(b_sb[t][:], bank[:])
-            b_ps.append(bank)
+            b_bank[t] = score("b_ps%d" % t, tag, b_sb[t], cb_codes, cb_scales, t, 0, S)
+
+        score_a(0, "bank5", *FIRST)
+        score_a(0, "bank6", *SECOND)
+        score_a(1, "bank0", 0, S)
+        cb_codes = pick_dealt_codes("cb_codes", cb_sb, "z_woven1")
+        score_b(0, "bank7")
+        score_b(1, "bank1")
 
         out_rows = out.rearrange("(p t) j -> p t j", t=PACK)
         a_n2 = [sb.tile([P, S], F32, name="a_n2_%d" % t) for t in range(PACK)]
@@ -260,48 +248,42 @@ def tile_picked_ccmpmaxbtwicp_none_p_kernel(
         def fetch_b(t, lo, hi):
             nc.vector.tensor_copy(b_n3[t][:, lo:hi], b_sb[t][:].indirect(entries(n3_sb, lo, hi)))
 
-        def take_lower(t, lo, hi):
-            nc.vector.scalar_tensor_tensor(
-                lower[t][:, lo:hi], b_ps[t][:, lo:hi], SIXTEENTH, a_n2[t][:, lo:hi], ALU.mult, ALU.min
-            )
-
         def take_upper(t, lo, hi):
-            for start, stop, bank in a_ps[t]:
+            for start, stop, bank in a_banks[t]:
                 c0, c1 = max(lo, start), min(hi, stop)
                 nc.vector.scalar_tensor_tensor(
                     upper[t][:, c0:c1], bank[:, c0 - start : c1 - start], SIXTEENTH, b_n3[t][:, c0:c1], ALU.mult, ALU.max
                 )
+
+        def take_lower(t, lo, hi):
+            nc.vector.scalar_tensor_tensor(
+                lower[t][:, lo:hi], b_bank[t][:, lo:hi], SIXTEENTH, a_n2[t][:, lo:hi], ALU.mult, ALU.min
+            )
 
         def finish(engine, op, in0, in1, tag, t, lo, hi):
             result = sb.tile([P, hi - lo], F32, name="result%d_%d" % (t, lo), tag=tag)
             engine.tensor_tensor(result[:], in0[:, lo:hi], in1[:, lo:hi], op)
             nc.sync.dma_start(out_rows[:, t, lo:hi], result[:])
 
-        score_a(1, "bank0")
-        cb_codes = pick_dealt_codes("cb_codes", cb_sb, "z_woven1")
-        score_b(0, "bank7")
-        score_b(1, "bank1")
-        for t in range(2):
+        for t in (0, 1):
             for lo, hi in HALVES:
                 fetch_a(t, lo, hi)
         excess = []
-        for t in range(2):
+        for t in (0, 1):
             gap = sb.tile([P, S], F32, name="gap%d" % t)
             nc.gpsimd.tensor_tensor(gap[:], a_n2[t][:], b_sb[t][:], ALU.subtract)
-            above = sb.tile([P, S], F32, name="excess%d" % t)
-            nc.scalar.activation(above[:], gap[:], ACT.Relu)
-            excess.append(above)
-        for t in range(2):
+            excess.append(sb.tile([P, S], F32, name="excess%d" % t))
+            nc.scalar.activation(excess[t][:], gap[:], ACT.Relu)
+        for t in (0, 1):
             for lo, hi in HALVES:
                 fetch_b(t, lo, hi)
             take_upper(t, 0, S)
             rest = sb.tile([P, S], F32, name="rest%d" % t, tag="rest%d" % t)
             nc.gpsimd.tensor_tensor(rest[:], upper[t][:], a_n2[t][:], ALU.subtract)
             finish(nc.gpsimd, ALU.add, rest, excess[t], "result%d" % t, t, 0, S)
-            score_a(t + 2, ("bank7", "bank1")[t])
+            score_a(t + 2, ("bank7", "bank1")[t], 0, S)
             score_b(t + 2, ("bank2", "bank3")[t])
 
-        first, second = HALVES
         for lo, hi in HALVES:
             fetch_a(2, lo, hi)
         for lo, hi in HALVES:
@@ -310,13 +292,13 @@ def tile_picked_ccmpmaxbtwicp_none_p_kernel(
         take_upper(2, 0, S)
         finish(nc.gpsimd, ALU.subtract, upper[2], lower[2], "rest1", 2, 0, S)
 
-        fetch_b(last, *first)
-        fetch_a(last, *first)
-        fetch_b(last, *second)
-        take_upper(last, *first)
-        take_lower(last, *first)
-        finish(nc.gpsimd, ALU.subtract, upper[last], lower[last], "lower2", last, *first)
-        fetch_a(last, *second)
-        take_upper(last, *second)
-        take_lower(last, *second)
-        finish(nc.vector, ALU.subtract, upper[last], lower[last], "result_last", last, *second)
+        fetch_b(LAST, *FIRST)
+        fetch_a(LAST, *FIRST)
+        fetch_b(LAST, *SECOND)
+        take_upper(LAST, *FIRST)
+        take_lower(LAST, *FIRST)
+        finish(nc.gpsimd, ALU.subtract, upper[LAST], lower[LAST], "lower2", LAST, *FIRST)
+        fetch_a(LAST, *SECOND)
+        take_upper(LAST, *SECOND)
+        take_lower(LAST, *SECOND)
+        finish(nc.vector, ALU.subtract, upper[LAST], lower[LAST], "result_last", LAST, *SECOND)

from contextlib import ExitStack

import concourse.mybir as mybir

K, T, S = 512, 2048, 512
FLOPS = 3 * 2 * K * S * S

F32 = mybir.dt.float32
BF16 = mybir.dt.bfloat16
I32 = mybir.dt.int32
U32 = mybir.dt.uint32
U16 = mybir.dt.uint16
U8 = mybir.dt.uint8
FP8X4 = mybir.dt.float8_e4m3fn_x4
ALU = mybir.AluOpType
ACT = mybir.ActivationFunctionType

P = 128
PACK = 4
LAST = PACK - 1
GROUP = 16
FIRST, SECOND = HALVES = ((0, S // 2), (S // 2, S))
SIXTEENTH = 0.0625


def tile_picked_ccmpmaxbtwicp_none_p_kernel(
    tc, x_words, x_scales, w1, gs, offs, n1, ca, cb, n2, n3, out
):
    nc = tc.nc
    with ExitStack() as ctx:
        lists = ctx.enter_context(tc.tile_pool(name="lists", bufs=1))
        sb = ctx.enter_context(tc.tile_pool(name="sb", bufs=1))
        psum = ctx.enter_context(tc.psum_pool(name="psum", bufs=1))

        def load_list(name, src):
            list_sb = lists.tile([P, S // GROUP], U16, name=name)
            nc.sync.dma_start(list_sb[:], src)
            return list_sb

        def entries(list_sb, lo, hi):
            return list_sb[:, lo // GROUP : hi // GROUP]

        def load_w(h):
            lo, hi = HALVES[h]
            raw = sb.tile([P, PACK, hi - lo], F32, name="w_raw%d" % h)
            nc.sync.dma_start(raw[:], w1.rearrange("(p j) c -> p j c", j=PACK)[:, :, lo:hi])
            return raw

        offs_sb = load_list("offs_sb", offs)
        w_raw = [load_w(0)]
        x_plane = sb.tile([P, T], U8, name="x_plane", align_bytes=64)
        nc.gpsimd.memset(x_plane[:, : T // 2].bitcast(I32), 0)
        nc.vector.memset(x_plane[:, T // 2 :].bitcast(I32), 0)
        for q in range(4):
            (nc.sync if q % 2 else nc.scalar).dma_start(
                x_plane[32 * q : 32 * q + 4, :].bitcast(I32), x_scales[0, 4 * q : 4 * q + 4, :].bitcast(I32)
            )
        warm = sb.tile([P, 2], F32, name="warm")
        nc.vector.memset(warm[:, 0:1], 0.0)
        nc.scalar.activation(warm[:, 1:2], warm[:, 0:1], ACT.Sigmoid)
        w_raw.append(load_w(1))
        ca_sb = load_list("ca_sb", ca)
        x_codes = sb.tile([P, T], U32, name="x_codes", align_bytes=64)
        nc.sync.dma_start(x_codes[:].bitcast(I32), x_words[0].rearrange("p n t -> p (n t)").bitcast(I32))
        n1_sb = load_list("n1_sb", n1)
        cb_sb = load_list("cb_sb", cb)
        gs_sb = sb.tile([P, PACK], F32, name="gs_sb")
        nc.sync.dma_start(gs_sb[:], gs.rearrange("(p t) one -> p (t one)", t=PACK))
        n2_sb = load_list("n2_sb", n2)
        n3_sb = load_list("n3_sb", n3)

        def pick_scales(name, list_sb, tag):
            picked = sb.tile([P, S], U8, name=name, tag=tag, align_bytes=64)
            nc.vector.tensor_copy(picked[:], x_plane[:].indirect(list_sb[:]))
            return picked

        def deal_scales(name, picked, tag):
            dealt = sb.tile([P, S], U8, name=name, tag=tag, align_bytes=64)
            nc.vector.tensor_copy(
                dealt[:].rearrange("p (t m) -> p t m", t=PACK), picked[:].rearrange("p (m t) -> p t m", t=PACK)
            )
            return dealt

        def pick_dealt_codes(name, list_sb, tag):
            dealt = sb.tile([P, S], U32, name=name, tag=tag, align_bytes=64)
            nc.vector.tensor_copy(dealt[:].rearrange("p (t m) -> p m t", t=PACK), x_codes[:].indirect(list_sb[:]))
            return dealt

        xq_scales = pick_scales("xq_scales", offs_sb, "xq_scales")
        ca_picked = pick_scales("ca_picked", ca_sb, "ca_picked")

        w_bf = [sb.tile([P, 2, P, PACK], BF16, name="w_bf%d" % u, align_bytes=64) for u in range(2)]
        for h, (lo, hi) in enumerate(HALVES):
            for u in range(2):
                nc.scalar.copy(
                    w_bf[u][:, :, lo // PACK : hi // PACK, :].rearrange("p t m j -> p m j t"),
                    w_raw[h][:].rearrange("p j (m t) -> p m j t", t=PACK)[:, :, :, 2 * u : 2 * u + 2],
                )
        w_mx = []
        for t in range(PACK):
            w_codes = sb.tile([P, P], U32, name="w_codes%d" % t, tag="w_codes%d" % t, align_bytes=64)
            w_scales = sb.tile([P, P], U8, name="w_scales%d" % t, align_bytes=64)
            nc.vector.quantize_mx(
                w_codes[:].bitcast(FP8X4), w_scales[:], w_bf[t // 2][:, t % 2].rearrange("p m j -> p (m j)")
            )
            w_mx.append((w_codes, w_scales))

        xq_codes = []
        for h, (lo, hi) in enumerate(HALVES):
            half = sb.tile([P, hi - lo], U32, name="xq_codes%d" % h, align_bytes=64)
            nc.vector.tensor_copy(half[:], x_codes[:].indirect(entries(offs_sb, lo, hi)))
            xq_codes.append(half)
        y_sb = [sb.tile([P, S], F32, name="y_sb%d" % t) for t in range(PACK)]

        def project(tag, t, start, stop):
            bank = psum.tile([P, stop - start], F32, name="y_ps%d_%d" % (t, start), tag=tag)
            w_codes, w_scales = w_mx[t]
            for h, (lo, hi) in enumerate(HALVES):
                if start <= lo and hi <= stop:
                    nc.tensor.matmul_mx(
                        bank[:, lo - start : hi - start], w_codes[:].bitcast(FP8X4), w_scales[:],
                        xq_codes[h][:].bitcast(FP8X4), xq_scales[:, lo:hi], start=True, stop=True,
                    )
            return bank

        y0_banks = [project("bank0", 0, *FIRST), project("bank1", 0, *SECOND)]
        y1_bank = project("bank2", 1, 0, S)
        for (lo, hi), bank in zip(HALVES, y0_banks):
            nc.scalar.copy(y_sb[0][:, lo:hi], bank[:])

        ca_codes = pick_dealt_codes("ca_codes", ca_sb, "ca_codes")
        nc.vector.tensor_copy(y_sb[1][:], y1_bank[:])
        ca_scales = deal_scales("ca_scales", ca_picked, "w_codes0")
        cb_picked = pick_scales("cb_picked", cb_sb, "w_codes1")
        cb_scales = deal_scales("cb_scales", cb_picked, "cb_scales")
        later_banks = {2: project("bank1", 2, 0, S), 3: project("bank2", 3, 0, S)}

        st = [sb.tile([P, S], F32, name="st%d" % t) for t in range(PACK)]
        for t in range(PACK):
            gate = sb.tile([P, S], F32, name="gate%d" % t)
            for lo, hi in HALVES:
                nc.scalar.activation(gate[:, lo:hi], y_sb[t][:].indirect(entries(n1_sb, lo, hi)), ACT.Sigmoid)
                nc.gpsimd.tensor_tensor(st[t][:, lo:hi], y_sb[t][:, lo:hi], gate[:, lo:hi], ALU.mult)
                if lo == 0 and t + 1 in later_banks:
                    nc.scalar.copy(y_sb[t + 1][:], later_banks[t + 1][:])

        st_n1 = [sb.tile([P, S], F32, name="st_n1_%d" % t) for t in range(PACK)]
        larger = [sb.tile([P, S], F32, name="larger%d" % t) for t in range(PACK)]
        z_rows = sb.tile([P, S // P, PACK, P], BF16, name="z_rows")

        def fetch_st(t, lo, hi):
            nc.vector.tensor_copy(st_n1[t][:, lo:hi], st[t][:].indirect(entries(n1_sb, lo, hi)))

        def take_larger(t, lo, hi):
            nc.vector.tensor_tensor(larger[t][:, lo:hi], st_n1[t][:, lo:hi], st[t][:, lo:hi], ALU.max)

        def z_rows_of(t, lo, hi):
            return z_rows[:, lo // P : hi // P, t, :]

        def larger_of(t, lo, hi):
            return larger[t][:, lo:hi].rearrange("p (c i) -> p c i", i=P)

        for t in range(LAST):
            for lo, hi in HALVES:
                fetch_st(t, lo, hi)
            for lo, hi in HALVES:
                take_larger(t, lo, hi)
        for t in range(LAST):
            nc.scalar.activation(z_rows_of(t, 0, S), larger_of(t, 0, S), ACT.Copy, scale=gs_sb[:, t : t + 1])

        def scale_last(lo, hi):
            nc.vector.tensor_scalar(
                z_rows_of(LAST, lo, hi), larger_of(LAST, lo, hi), gs_sb[:, LAST : LAST + 1], None, ALU.mult
            )

        z_codes = sb.tile([P, S], U32, name="z_codes", align_bytes=64)
        z_scales = sb.tile([P, S], U8, name="z_scales", align_bytes=64)
        woven = [
            sb.tile([P, 2, P * PACK], BF16, name="z_woven%d" % h, tag="z_woven%d" % h, align_bytes=64) for h in range(2)
        ]

        def weave(copy, block):
            copy(
                woven[block // 2][:, block % 2].rearrange("p (g i t) -> p g t i", i=4, t=PACK),
                z_rows[:, block].rearrange("p t (g i) -> p g t i", i=4),
            )

        def quantize_z(h):
            lo, hi = HALVES[h]
            nc.vector.quantize_mx(
                z_codes[:, lo:hi].bitcast(FP8X4), z_scales[:, lo:hi], woven[h][:].rearrange("p b w -> p (b w)")
            )

        third, fourth = (S // 2, 3 * S // 4), (3 * S // 4, S)
        fetch_st(LAST, *FIRST)
        fetch_st(LAST, *third)
        take_larger(LAST, *FIRST)
        fetch_st(LAST, *fourth)
        scale_last(*FIRST)
        take_larger(LAST, *third)
        take_larger(LAST, *fourth)
        weave(nc.scalar.copy, 0)
        weave(nc.vector.tensor_copy, 1)
        scale_last(*SECOND)
        quantize_z(0)
        weave(nc.scalar.copy, 2)
        weave(nc.vector.tensor_copy, 3)
        quantize_z(1)

        a_sb = [sb.tile([P, S], F32, name="a_sb%d" % t) for t in range(PACK)]
        b_sb = [sb.tile([P, S], F32, name="b_sb%d" % t) for t in range(PACK)]
        a_banks = [[] for t in range(PACK)]
        b_bank = {}

        def score(name, tag, window, codes, scales, t, lo, hi):
            cols = slice(t * P, (t + 1) * P)
            bank = psum.tile([P, hi - lo], F32, name=name, tag=tag)
            nc.tensor.matmul_mx(
                bank[:], codes[:, cols].bitcast(FP8X4), scales[:, cols],
                z_codes[:, lo:hi].bitcast(FP8X4), z_scales[:, lo:hi], start=True, stop=True,
            )
            nc.scalar.activation(window[:, lo:hi], bank[:], ACT.Copy, scale=SIXTEENTH)
            return bank

        def score_a(t, tag, lo, hi):
            bank = score("a_ps%d_%d" % (t, lo), tag, a_sb[t], ca_codes, ca_scales, t, lo, hi)
            a_banks[t].append((lo, hi, bank))

        def score_b(t, tag):
            b_bank[t] = score("b_ps%d" % t, tag, b_sb[t], cb_codes, cb_scales, t, 0, S)

        score_a(0, "bank5", *FIRST)
        score_a(0, "bank6", *SECOND)
        score_a(1, "bank0", 0, S)
        cb_codes = pick_dealt_codes("cb_codes", cb_sb, "z_woven1")
        score_b(0, "bank7")
        score_b(1, "bank1")

        out_rows = out.rearrange("(p t) j -> p t j", t=PACK)
        a_n2 = [sb.tile([P, S], F32, name="a_n2_%d" % t) for t in range(PACK)]
        b_n3 = [sb.tile([P, S], F32, name="b_n3_%d" % t) for t in range(PACK)]
        upper = [sb.tile([P, S], F32, name="upper%d" % t) for t in range(PACK)]
        lower = {t: sb.tile([P, S], F32, name="lower%d" % t, tag="lower%d" % t) for t in (2, 3)}

        def fetch_a(t, lo, hi):
            nc.vector.tensor_copy(a_n2[t][:, lo:hi], a_sb[t][:].indirect(entries(n2_sb, lo, hi)))

        def fetch_b(t, lo, hi):
            nc.vector.tensor_copy(b_n3[t][:, lo:hi], b_sb[t][:].indirect(entries(n3_sb, lo, hi)))

        def take_upper(t, lo, hi):
            for start, stop, bank in a_banks[t]:
                c0, c1 = max(lo, start), min(hi, stop)
                nc.vector.scalar_tensor_tensor(
                    upper[t][:, c0:c1], bank[:, c0 - start : c1 - start], SIXTEENTH, b_n3[t][:, c0:c1], ALU.mult, ALU.max
                )

        def take_lower(t, lo, hi):
            nc.vector.scalar_tensor_tensor(
                lower[t][:, lo:hi], b_bank[t][:, lo:hi], SIXTEENTH, a_n2[t][:, lo:hi], ALU.mult, ALU.min
            )

        def finish(engine, op, in0, in1, tag, t, lo, hi):
            result = sb.tile([P, hi - lo], F32, name="result%d_%d" % (t, lo), tag=tag)
            engine.tensor_tensor(result[:], in0[:, lo:hi], in1[:, lo:hi], op)
            nc.sync.dma_start(out_rows[:, t, lo:hi], result[:])

        for t in (0, 1):
            for lo, hi in HALVES:
                fetch_a(t, lo, hi)
        excess = []
        for t in (0, 1):
            gap = sb.tile([P, S], F32, name="gap%d" % t)
            nc.gpsimd.tensor_tensor(gap[:], a_n2[t][:], b_sb[t][:], ALU.subtract)
            excess.append(sb.tile([P, S], F32, name="excess%d" % t))
            nc.scalar.activation(excess[t][:], gap[:], ACT.Relu)
        for t in (0, 1):
            for lo, hi in HALVES:
                fetch_b(t, lo, hi)
            take_upper(t, 0, S)
            rest = sb.tile([P, S], F32, name="rest%d" % t, tag="rest%d" % t)
            nc.gpsimd.tensor_tensor(rest[:], upper[t][:], a_n2[t][:], ALU.subtract)
            finish(nc.gpsimd, ALU.add, rest, excess[t], "result%d" % t, t, 0, S)
            score_a(t + 2, ("bank7", "bank1")[t], 0, S)
            score_b(t + 2, ("bank2", "bank3")[t])

        for lo, hi in HALVES:
            fetch_a(2, lo, hi)
        for lo, hi in HALVES:
            fetch_b(2, lo, hi)
        take_lower(2, 0, S)
        take_upper(2, 0, S)
        finish(nc.gpsimd, ALU.subtract, upper[2], lower[2], "rest1", 2, 0, S)

        fetch_b(LAST, *FIRST)
        fetch_a(LAST, *FIRST)
        fetch_b(LAST, *SECOND)
        take_upper(LAST, *FIRST)
        take_lower(LAST, *FIRST)
        finish(nc.gpsimd, ALU.subtract, upper[LAST], lower[LAST], "lower2", LAST, *FIRST)
        fetch_a(LAST, *SECOND)
        take_upper(LAST, *SECOND)
        take_lower(LAST, *SECOND)
        finish(nc.vector, ALU.subtract, upper[LAST], lower[LAST], "result_last", LAST, *SECOND)
